import numpy as np
import ml_dtypes


def mxq(x, axis, fmt="e4m3"):
    dtype, down = {"e4m3": (ml_dtypes.float8_e4m3fn, 7), "e5m2": (ml_dtypes.float8_e5m2, 14)}[fmt]
    v = np.moveaxis(np.asarray(x, np.float32).astype(ml_dtypes.bfloat16).astype(np.float64), axis, -1)
    blocks = v.reshape(v.shape[:-1] + (-1, 32))
    amax = np.abs(blocks).max(-1, keepdims=True)
    byte = np.maximum(np.where(amax > 0, np.frexp(amax)[1] - 1 + 127, 0) - down, 1)
    scale = np.exp2(byte - 127.0)
    codes = (blocks / scale).astype(np.float32).astype(dtype).astype(np.float64)
    return np.moveaxis((codes * scale).reshape(v.shape), -1, axis)


WIDE = False


def mx_kscale(k):
    if not WIDE:
        return np.ones(k)
    levels = np.array([30, -30])
    if k % 512:
        return np.exp2(np.random.permutation(np.resize(levels, k // 32))).repeat(32)
    a = np.empty((k // 512, 16))
    for p in range(k // 512):
        a[p, :8] = np.random.permutation(np.resize(levels, 8))
        for g in range(8):
            far = levels[np.abs(levels - a[p, g]) >= 10]
            a[p, g + 8] = far[np.random.randint(len(far))]
    return np.exp2(a.ravel()).repeat(32)


def f64(x):
    return np.asarray(x).astype(np.float64)


def striped(idx):
    return np.tile(np.asarray(idx).reshape(-1, 16).T, (8, 1)).astype(np.uint16)


def unstriped(offs):
    return offs[:16].T.reshape(-1).astype(np.int64)


E2M1 = np.array([0.0, 0.5, 1.0, 1.5, 2.0, 3.0, 4.0, 6.0, -0.0, -0.5, -1.0, -1.5, -2.0, -3.0, -4.0, -6.0])


def pack_weight(w, fmt):
    k, n = w.shape
    w = f64(np.asarray(w, np.float32).astype(ml_dtypes.bfloat16)).reshape(k // 32, 32, n)
    amax = np.abs(w).max(1)
    if fmt in ("e4m3", "e5m2"):
        byte = np.frexp(amax)[1] - 1 + 127 - (7 if fmt == "e4m3" else 14)
    else:
        mant, ex = np.frexp(amax / 6.0)
        byte = np.where(mant > 0.5, ex, ex - 1) + 127
    byte = np.clip(np.where(amax > 0, byte, 1), 1, 254)
    scaled = (w * np.exp2(127.0 - byte)[:, None, :]).reshape(k, n).astype(np.float32)
    by_word = np.ascontiguousarray(scaled.reshape(k // 512, 128, 4, n).transpose(0, 1, 3, 2))
    if fmt in ("e4m3", "e5m2"):
        words = by_word.astype(ml_dtypes.float8_e4m3fn if fmt == "e4m3" else ml_dtypes.float8_e5m2).view(np.uint8)
    else:
        c = by_word.astype(ml_dtypes.float4_e2m1fn).view(np.uint8) & 0xF
        words = (c[..., 0::2] | (c[..., 1::2] << 4)).reshape(k // 512, 128, 2 * n)
    return np.ascontiguousarray(words), np.ascontiguousarray(byte.astype(np.uint8).reshape(k // 512, 16, n))


def unpack_weight(words, scales, fmt):
    g, _, n = scales.shape
    words = np.ascontiguousarray(words).reshape(g, 128, n, -1)
    if fmt in ("e4m3", "e5m2"):
        vals = words.view(ml_dtypes.float8_e4m3fn if fmt == "e4m3" else ml_dtypes.float8_e5m2).astype(np.float64)
    else:
        nib = np.empty((g, 128, n, 4), np.uint8)
        nib[..., 0::2] = words & 0xF
        nib[..., 1::2] = words >> 4
        vals = E2M1[nib]
    vals = vals * np.repeat(np.exp2(scales.astype(np.float64) - 127.0), 8, axis=1)[..., None]
    return vals.transpose(0, 1, 3, 2).reshape(g * 512, n)


def e4m3fn_bytes(y):
    return np.clip(np.asarray(y, np.float64), -448.0, 448.0).astype(np.float32).astype(ml_dtypes.float8_e4m3fn).view(np.uint8)


def e4m3fn_values(b):
    return np.asarray(b, np.uint8).view(ml_dtypes.float8_e4m3fn).astype(np.float64)


K, T, J, R, F, Z, C, V, I, N = 512, 1024, 256, 512, 512, 1024, 512, 1024, 256, 256


def setup_inputs():
    n = np.random.standard_normal
    idx = np.random.permutation(T)[:J]
    idx2 = np.random.permutation(Z)[:J]
    idx3 = np.random.permutation(V)[:I]
    idx4 = np.random.permutation(C)[:I]
    idx5 = np.random.permutation(C)[:J]
    fk = mx_kscale(K)
    ff = mx_kscale(F)
    fr = mx_kscale(R)
    xtp = pack_weight(n((K, T)) / fk[:, None], "e4m3")
    xop = pack_weight(n((F, Z)) / ff[:, None], "e2m1")
    wp = pack_weight(n((K, R)) * 1 / np.sqrt(K) * fk[:, None] * fr, "e2m1")
    w0p = pack_weight(n((F, R)) * 1 / np.sqrt(F) * ff[:, None] * fr, "e5m2")
    wbp = pack_weight(n((R, N)) * 1 / np.sqrt(R) / fr[:, None], "e5m2")
    return {
        "xt_words": xtp[0],
        "xt_scales": xtp[1],
        "xo_words": xop[0],
        "xo_scales": xop[1],
        "w_words": wp[0],
        "w_scales": wp[1],
        "w0_words": w0p[0],
        "w0_scales": w0p[1],
        "ca": e4m3fn_bytes(60.0 * n((R, V))),
        "st": (np.random.uniform(0.008, 0.024, (R, 1)) * fr[:, None]).astype(np.float32),
        "wb_words": wbp[0],
        "wb_scales": wbp[1],
        "offs": striped(idx),
        "offs2": striped(idx2),
        "offs3": striped(idx3),
        "offs4": striped(idx4),
        "offs5": striped(idx5),
    }


def reference(xt_words, xt_scales, xo_words, xo_scales, w_words, w_scales, w0_words, w0_scales, ca, st, wb_words, wb_scales, offs, offs2, offs3, offs4, offs5):
    idx = unstriped(offs)
    idx2 = unstriped(offs2)
    idx3 = unstriped(offs3)
    idx4 = unstriped(offs4)
    idx5 = unstriped(offs5)
    xtu = unpack_weight(xt_words, xt_scales, "e4m3")
    xou = unpack_weight(xo_words, xo_scales, "e2m1")
    wu = unpack_weight(w_words, w_scales, "e2m1")
    w0u = unpack_weight(w0_words, w0_scales, "e5m2")
    wbu = unpack_weight(wb_words, wb_scales, "e5m2")
    xtidxg = xtu[:, idx]
    xoidx2g = xou[:, idx2]
    a = wu.T @ xtidxg + w0u.T @ xoidx2g
    g1 = e4m3fn_values(ca)[:, idx3] * f64(st)
    pw = np.zeros((R, C))
    pw[:, idx4] = g1
    hid = np.maximum(a - pw[:, idx5], 0.0)
    hidq = mxq(hid, 0, "e4m3")
    p = wbu.T @ hidq
    return p

@@ -1,0 +1,180 @@
+from contextlib import ExitStack
+
+import concourse.mybir as mybir
+from concourse.masks import make_identity
+
+K, T, J, R, F, Z, C, V, I, N = 512, 1024, 256, 512, 512, 1024, 512, 1024, 256, 256
+FLOPS = 2 * K * R * J + 2 * F * R * J + 2 * R * N * J
+
+F32 = mybir.dt.float32
+BF16 = mybir.dt.bfloat16
+I32 = mybir.dt.int32
+U32 = mybir.dt.uint32
+U16 = mybir.dt.uint16
+U8 = mybir.dt.uint8
+FP8 = mybir.dt.float8_e4m3fn
+E4M3 = mybir.dt.float8_e4m3fn_x4
+E5M2 = mybir.dt.float8_e5m2_x4
+E2M1 = mybir.dt.float4_e2m1fn_x4
+RELU = mybir.ActivationFunctionType.Relu
+COPY = mybir.ActivationFunctionType.Copy
+ALU = mybir.AluOpType
+
+P = 128
+PACK = 4
+
+
+def tile_list_postedcodes_kernel(
+    tc, xt_words, xt_scales, xo_words, xo_scales, w_words, w_scales, w0_words, w0_scales,
+    ca, st, wb_words, wb_scales, offs, offs2, offs3, offs4, offs5, out,
+):
+    nc = tc.nc
+    with ExitStack() as ctx:
+        sb = ctx.enter_context(tc.tile_pool(name="sb", bufs=1))
+        ps = ctx.enter_context(tc.psum_pool(name="ps", bufs=1))
+
+        def tile(shape, dtype, name):
+            return sb.tile(shape, dtype, name=name, align_bytes=64)
+
+        lists = {}
+        for name in ("l1", "l2", "l3", "l4", "l5"):
+            lists[name] = tile([P, J // 16], U16, name)
+        ca_sb = [tile([P, V], U8, "ca%d" % t) for t in range(PACK)]
+        st_sb = tile([P, PACK], F32, "st_sb")
+        xt_w = tile([P, T], I32, "xt_w")
+        xo_w = tile([P, Z], U16, "xo_w")
+        w_w = tile([P, 2 * R], U8, "w_w")
+        w0_w = tile([P, R], I32, "w0_w")
+        wb_w = tile([P, N], I32, "wb_w")
+        xt_s = tile([P, T], U8, "xt_s")
+        xo_s = tile([P, Z], U8, "xo_s")
+        w_s = tile([P, R], U8, "w_s")
+        w0_s = tile([P, R], U8, "w0_s")
+        wb_s = tile([P, N], U8, "wb_s")
+        board = [tile([P, C], F32, "board%d" % t) for t in range(PACK)]
+        ident = tile([P, P], F32, "ident")
+
+        for plane in (xt_s, xo_s):
+            nc.vector.memset(plane[:].bitcast(I32), 0)
+        for t in range(PACK):
+            engine = nc.vector if t < 2 else nc.gpsimd
+            engine.memset(board[t][:], 0.0)
+        make_identity(nc, ident[:])
+
+        def load_scales(plane, src, quadrants):
+            for q in quadrants:
+                nc.sync.dma_start(plane[32 * q : 32 * q + 4, :].bitcast(I32), src[0, 4 * q : 4 * q + 4, :].bitcast(I32))
+
+        ca_rows = ca.rearrange("(p t) v -> p t v", t=PACK)
+        nc.sync.dma_start(lists["l3"][:], offs3)
+        nc.sync.dma_start(ca_sb[0][:], ca_rows[:, 0, :])
+        nc.sync.dma_start(st_sb[:], st.rearrange("(p t) o -> p (t o)", t=PACK))
+        nc.sync.dma_start(lists["l4"][:], offs4)
+        nc.sync.dma_start(ca_sb[1][:], ca_rows[:, 1, :])
+        nc.sync.dma_start(lists["l1"][:], offs)
+        nc.sync.dma_start(xt_w[:], xt_words[0].rearrange("p c r -> p (c r)").bitcast(I32))
+        load_scales(xt_s, xt_scales, range(4))
+        nc.sync.dma_start(ca_sb[2][:], ca_rows[:, 2, :])
+        nc.sync.dma_start(lists["l2"][:], offs2)
+        nc.sync.dma_start(xo_w[:].bitcast(I32), xo_words[0].bitcast(I32))
+        load_scales(xo_s, xo_scales, range(4))
+        nc.sync.dma_start(ca_sb[3][:], ca_rows[:, 3, :])
+        nc.sync.dma_start(w_w[:].bitcast(I32), w_words[0].bitcast(I32))
+        load_scales(w_s, w_scales, range(4))
+        nc.sync.dma_start(w0_w[:], w0_words[0].rearrange("p c r -> p (c r)").bitcast(I32))
+        load_scales(w0_s, w0_scales, range(4))
+        nc.sync.dma_start(wb_w[:], wb_words[0].rearrange("p c r -> p (c r)").bitcast(I32))
+        load_scales(wb_s, wb_scales, range(2))
+        nc.sync.dma_start(lists["l5"][:], offs5)
+        load_scales(wb_s, wb_scales, range(2, 4))
+
+        codes = [tile([P, I], U8, "codes%d" % t) for t in range(PACK)]
+        bars = [tile([P, I], F32, "bars%d" % t) for t in range(PACK)]
+        picked = [tile([P, J], F32, "picked%d" % t) for t in range(PACK)]
+        xt_wg = tile([P, J], U32, "xt_wg")
+        xt_sg = tile([P, J], U8, "xt_sg")
+        xo_wg = tile([P, J], U16, "xo_wg")
+        xo_sg = tile([P, J], U8, "xo_sg")
+
+        def look_up(t):
+            nc.vector.tensor_copy(codes[t][:], ca_sb[t][:].indirect(lists["l3"][:]))
+
+        def post_scalar(t):
+            nc.scalar.activation(bars[t][:], codes[t][:].bitcast(FP8), COPY, scale=st_sb[:, t : t + 1])
+            nc.scalar.activation(board[t][:].indirect(lists["l4"][:]), bars[t][:], COPY)
+
+        def post_vector(t):
+            nc.vector.tensor_scalar(bars[t][:], codes[t][:].bitcast(FP8), st_sb[:, t : t + 1], None, ALU.mult)
+            nc.vector.tensor_copy(board[t][:].indirect(lists["l4"][:]), bars[t][:])
+
+        look_up(0)
+        post_scalar(0)
+        look_up(1)
+        post_scalar(1)
+        nc.vector.tensor_copy(xt_wg[:], xt_w[:].bitcast(U32).indirect(lists["l1"][:]))
+        nc.vector.tensor_copy(xt_sg[:], xt_s[:].indirect(lists["l1"][:]))
+        look_up(2)
+        post_scalar(2)
+        nc.vector.tensor_copy(xo_wg[:], xo_w[:].indirect(lists["l2"][:]))
+        nc.vector.tensor_copy(xo_sg[:], xo_s[:].indirect(lists["l2"][:]))
+        look_up(3)
+        post_vector(3)
+
+        a_rows = [ps.tile([P, J], F32, name="a_rows%d" % t) for t in range(PACK)]
+        halves = range(J // P)
+        a_slots = [ps.tile([P, R], F32, name="a_slots%d" % h) for h in halves]
+        for h in halves:
+            cols = slice(h * P, (h + 1) * P)
+            nc.tensor.matmul_mx(
+                out=a_slots[h][:], lhsT=xt_wg[:, cols].bitcast(E4M3), lhsT_scale=xt_sg[:, cols],
+                rhs=w_w[:].bitcast(E2M1), rhs_scale=w_s[:], start=True, stop=False,
+            )
+        for h in halves:
+            cols = slice(h * P, (h + 1) * P)
+            nc.tensor.matmul_mx(
+                out=a_slots[h][:], lhsT=xo_wg[:, cols].bitcast(E2M1), lhsT_scale=xo_sg[:, cols],
+                rhs=w0_w[:].bitcast(E5M2), rhs_scale=w0_s[:], start=False, stop=True,
+            )
+        dealt = [tile([P, PACK, P], F32, "dealt%d" % h) for h in halves]
+        nc.vector.tensor_copy(dealt[0][:], a_slots[0][:].rearrange("j (p t) -> j t p", t=PACK))
+        nc.scalar.copy(dealt[1][:], a_slots[1][:].rearrange("j (p t) -> j t p", t=PACK))
+        for t in (3, 0, 1, 2):
+            for h in halves:
+                nc.tensor.transpose(a_rows[t][:, h * P : (h + 1) * P], dealt[h][:, t, :], ident[:])
+
+        diff = tile([P, PACK, J], F32, "diff")
+        for t, on_scalar in ((3, False), (0, True), (1, True), (2, True)):
+            window = board[t][:].indirect(lists["l5"][:])
+            if on_scalar:
+                nc.scalar.activation(picked[t][:], window, COPY)
+            else:
+                nc.vector.tensor_copy(picked[t][:], window)
+            nc.vector.tensor_tensor(diff[:, t, :], a_rows[t][:], picked[t][:], ALU.subtract)
+
+        hid = [tile([P, P, PACK], BF16, "hid%d" % h) for h in halves]
+        hid_w = [tile([P, P], U32, "hid_w%d" % h) for h in halves]
+        hid_s = [tile([P, P], U8, "hid_s%d" % h) for h in halves]
+        for h in halves:
+            woven = hid[h][:].rearrange("p (c i) t -> p c t i", i=4)
+            rows = diff[:, :, h * P : (h + 1) * P].rearrange("p t (c i) -> p c t i", i=4)
+            if h == 0:
+                nc.vector.tensor_scalar(woven, rows, 0.0, None, ALU.max)
+            else:
+                nc.scalar.activation(woven, rows, RELU)
+        for h in halves:
+            nc.vector.quantize_mx(out=hid_w[h][:].bitcast(E4M3), scales=hid_s[h][:], in_=hid[h][:].rearrange("p j t -> p (j t)"))
+        out_rows = out.rearrange("(g p) j -> p g j", p=P)
+        for h in halves:
+            acc = ps.tile([P, N // P, P], F32, name="acc%d" % h)
+            for g in range(N // P):
+                cols = slice(g * P, (g + 1) * P)
+                nc.tensor.matmul_mx(
+                    out=acc[:, g, :], lhsT=wb_w[:, cols].bitcast(E5M2), lhsT_scale=wb_s[:, cols],
+                    rhs=hid_w[h][:].bitcast(E4M3), rhs_scale=hid_s[h][:], start=True, stop=True,
+                )
+            res = tile([P, N // P, P], F32, "res%d" % h)
+            if h == 0:
+                nc.scalar.copy(res[:], acc[:])
+            else:
+                nc.vector.tensor_copy(res[:], acc[:])
+            nc.sync.dma_start(out_rows[:, :, h * P : (h + 1) * P], res[:])

@@ -68,8 +68,8 @@ def tile_list_postedcodes_kernel(
         ca_rows = ca.rearrange("(p t) v -> p t v", t=PACK)
         nc.sync.dma_start(lists["l3"][:], offs3)
         nc.sync.dma_start(ca_sb[0][:], ca_rows[:, 0, :])
-        nc.sync.dma_start(st_sb[:], st.rearrange("(p t) o -> p (t o)", t=PACK))
         nc.sync.dma_start(lists["l4"][:], offs4)
+        nc.sync.dma_start(st_sb[:], st.rearrange("(p t) o -> p (t o)", t=PACK))
         nc.sync.dma_start(ca_sb[1][:], ca_rows[:, 1, :])
         nc.sync.dma_start(lists["l1"][:], offs)
         nc.sync.dma_start(xt_w[:], xt_words[0].rearrange("p c r -> p (c r)").bitcast(I32))
@@ -79,18 +79,17 @@ def tile_list_postedcodes_kernel(
         nc.sync.dma_start(xo_w[:].bitcast(I32), xo_words[0].bitcast(I32))
         load_scales(xo_s, xo_scales, range(4))
         nc.sync.dma_start(ca_sb[3][:], ca_rows[:, 3, :])
+        nc.sync.dma_start(lists["l5"][:], offs5)
         nc.sync.dma_start(w_w[:].bitcast(I32), w_words[0].bitcast(I32))
         load_scales(w_s, w_scales, range(4))
         nc.sync.dma_start(w0_w[:], w0_words[0].rearrange("p c r -> p (c r)").bitcast(I32))
         load_scales(w0_s, w0_scales, range(4))
         nc.sync.dma_start(wb_w[:], wb_words[0].rearrange("p c r -> p (c r)").bitcast(I32))
-        load_scales(wb_s, wb_scales, range(2))
-        nc.sync.dma_start(lists["l5"][:], offs5)
-        load_scales(wb_s, wb_scales, range(2, 4))
+        load_scales(wb_s, wb_scales, range(4))
 
         codes = [tile([P, I], U8, "codes%d" % t) for t in range(PACK)]
         bars = [tile([P, I], F32, "bars%d" % t) for t in range(PACK)]
-        picked = [tile([P, J], F32, "picked%d" % t) for t in range(PACK)]
+        picked = tile([P, PACK, J], F32, "picked")
         xt_wg = tile([P, J], U32, "xt_wg")
         xt_sg = tile([P, J], U8, "xt_sg")
         xo_wg = tile([P, J], U16, "xo_wg")
@@ -100,12 +99,11 @@ def tile_list_postedcodes_kernel(
             nc.vector.tensor_copy(codes[t][:], ca_sb[t][:].indirect(lists["l3"][:]))
 
         def post_scalar(t):
-            nc.scalar.activation(bars[t][:], codes[t][:].bitcast(FP8), COPY, scale=st_sb[:, t : t + 1])
-            nc.scalar.activation(board[t][:].indirect(lists["l4"][:]), bars[t][:], COPY)
-
-        def post_vector(t):
-            nc.vector.tensor_scalar(bars[t][:], codes[t][:].bitcast(FP8), st_sb[:, t : t + 1], None, ALU.mult)
-            nc.vector.tensor_copy(board[t][:].indirect(lists["l4"][:]), bars[t][:])
+            if t == 0:
+                nc.scalar.activation(bars[t][:], codes[t][:].bitcast(FP8), COPY)
+            else:
+                nc.gpsimd.tensor_copy(bars[t][:], codes[t][:].bitcast(FP8))
+            nc.scalar.activation(board[t][:].indirect(lists["l4"][:]), bars[t][:], COPY, scale=st_sb[:, t : t + 1])
 
         look_up(0)
         post_scalar(0)
@@ -118,9 +116,9 @@ def tile_list_postedcodes_kernel(
         nc.vector.tensor_copy(xo_wg[:], xo_w[:].indirect(lists["l2"][:]))
         nc.vector.tensor_copy(xo_sg[:], xo_s[:].indirect(lists["l2"][:]))
         look_up(3)
-        post_vector(3)
+        post_scalar(3)
 
-        a_rows = [ps.tile([P, J], F32, name="a_rows%d" % t) for t in range(PACK)]
+        a_rows = [ps.tile([P, PACK, P], F32, name="a_rows%d" % h) for h in range(J // P)]
         halves = range(J // P)
         a_slots = [ps.tile([P, R], F32, name="a_slots%d" % h) for h in halves]
         for h in halves:
@@ -136,28 +134,25 @@ def tile_list_postedcodes_kernel(
                 rhs=w0_w[:].bitcast(E5M2), rhs_scale=w0_s[:], start=False, stop=True,
             )
         dealt = [tile([P, PACK, P], F32, "dealt%d" % h) for h in halves]
-        nc.vector.tensor_copy(dealt[0][:], a_slots[0][:].rearrange("j (p t) -> j t p", t=PACK))
-        nc.scalar.copy(dealt[1][:], a_slots[1][:].rearrange("j (p t) -> j t p", t=PACK))
-        for t in (3, 0, 1, 2):
-            for h in halves:
-                nc.tensor.transpose(a_rows[t][:, h * P : (h + 1) * P], dealt[h][:, t, :], ident[:])
+        for h in halves:
+            nc.vector.tensor_copy(dealt[h][:], a_slots[h][:].rearrange("j (p t) -> j t p", t=PACK))
+            for t in range(PACK):
+                nc.tensor.transpose(a_rows[h][:, t, :], dealt[h][:, t, :], ident[:])
 
-        diff = tile([P, PACK, J], F32, "diff")
-        for t, on_scalar in ((3, False), (0, True), (1, True), (2, True)):
-            window = board[t][:].indirect(lists["l5"][:])
-            if on_scalar:
-                nc.scalar.activation(picked[t][:], window, COPY)
-            else:
-                nc.vector.tensor_copy(picked[t][:], window)
-            nc.vector.tensor_tensor(diff[:, t, :], a_rows[t][:], picked[t][:], ALU.subtract)
+        for t in range(PACK - 1):
+            nc.vector.tensor_copy(picked[:, t, :], board[t][:].indirect(lists["l5"][:]))
+        nc.scalar.activation(picked[:, PACK - 1, :], board[PACK - 1][:].indirect(lists["l5"][:]), COPY)
+        diff = [tile([P, PACK, P], F32, "diff%d" % h) for h in halves]
+        for h in halves:
+            nc.vector.tensor_tensor(diff[h][:], a_rows[h][:], picked[:, :, h * P : (h + 1) * P], ALU.subtract)
 
         hid = [tile([P, P, PACK], BF16, "hid%d" % h) for h in halves]
         hid_w = [tile([P, P], U32, "hid_w%d" % h) for h in halves]
         hid_s = [tile([P, P], U8, "hid_s%d" % h) for h in halves]
         for h in halves:
             woven = hid[h][:].rearrange("p (c i) t -> p c t i", i=4)
-            rows = diff[:, :, h * P : (h + 1) * P].rearrange("p t (c i) -> p c t i", i=4)
-            if h == 0:
+            rows = diff[h][:].rearrange("p t (c i) -> p c t i", i=4)
+            if h == 1:
                 nc.vector.tensor_scalar(woven, rows, 0.0, None, ALU.max)
             else:
                 nc.scalar.activation(woven, rows, RELU)

from contextlib import ExitStack

import concourse.mybir as mybir
from concourse.masks import make_identity

K, T, J, R, F, Z, C, V, I, N = 512, 1024, 256, 512, 512, 1024, 512, 1024, 256, 256
FLOPS = 2 * K * R * J + 2 * F * R * J + 2 * R * N * J

F32 = mybir.dt.float32
BF16 = mybir.dt.bfloat16
I32 = mybir.dt.int32
U32 = mybir.dt.uint32
U16 = mybir.dt.uint16
U8 = mybir.dt.uint8
FP8 = mybir.dt.float8_e4m3fn
E4M3 = mybir.dt.float8_e4m3fn_x4
E5M2 = mybir.dt.float8_e5m2_x4
E2M1 = mybir.dt.float4_e2m1fn_x4
RELU = mybir.ActivationFunctionType.Relu
COPY = mybir.ActivationFunctionType.Copy
ALU = mybir.AluOpType

P = 128
PACK = 4


def tile_list_postedcodes_kernel(
    tc, xt_words, xt_scales, xo_words, xo_scales, w_words, w_scales, w0_words, w0_scales,
    ca, st, wb_words, wb_scales, offs, offs2, offs3, offs4, offs5, out,
):
    nc = tc.nc
    with ExitStack() as ctx:
        sb = ctx.enter_context(tc.tile_pool(name="sb", bufs=1))
        ps = ctx.enter_context(tc.psum_pool(name="ps", bufs=1))

        def tile(shape, dtype, name):
            return sb.tile(shape, dtype, name=name, align_bytes=64)

        lists = {}
        for name in ("l1", "l2", "l3", "l4", "l5"):
            lists[name] = tile([P, J // 16], U16, name)
        ca_sb = [tile([P, V], U8, "ca%d" % t) for t in range(PACK)]
        st_sb = tile([P, PACK], F32, "st_sb")
        xt_w = tile([P, T], I32, "xt_w")
        xo_w = tile([P, Z], U16, "xo_w")
        w_w = tile([P, 2 * R], U8, "w_w")
        w0_w = tile([P, R], I32, "w0_w")
        wb_w = tile([P, N], I32, "wb_w")
        xt_s = tile([P, T], U8, "xt_s")
        xo_s = tile([P, Z], U8, "xo_s")
        w_s = tile([P, R], U8, "w_s")
        w0_s = tile([P, R], U8, "w0_s")
        wb_s = tile([P, N], U8, "wb_s")
        board = [tile([P, C], F32, "board%d" % t) for t in range(PACK)]
        ident = tile([P, P], F32, "ident")

        for plane in (xt_s, xo_s):
            nc.vector.memset(plane[:].bitcast(I32), 0)
        for t in range(PACK):
            engine = nc.vector if t < 2 else nc.gpsimd
            engine.memset(board[t][:], 0.0)
        make_identity(nc, ident[:])

        def load_scales(plane, src, quadrants):
            for q in quadrants:
                nc.sync.dma_start(plane[32 * q : 32 * q + 4, :].bitcast(I32), src[0, 4 * q : 4 * q + 4, :].bitcast(I32))

        ca_rows = ca.rearrange("(p t) v -> p t v", t=PACK)
        nc.sync.dma_start(lists["l3"][:], offs3)
        nc.sync.dma_start(ca_sb[0][:], ca_rows[:, 0, :])
        nc.sync.dma_start(lists["l4"][:], offs4)
        nc.sync.dma_start(st_sb[:], st.rearrange("(p t) o -> p (t o)", t=PACK))
        nc.sync.dma_start(ca_sb[1][:], ca_rows[:, 1, :])
        nc.sync.dma_start(lists["l1"][:], offs)
        nc.sync.dma_start(xt_w[:], xt_words[0].rearrange("p c r -> p (c r)").bitcast(I32))
        load_scales(xt_s, xt_scales, range(4))
        nc.sync.dma_start(ca_sb[2][:], ca_rows[:, 2, :])
        nc.sync.dma_start(lists["l2"][:], offs2)
        nc.sync.dma_start(xo_w[:].bitcast(I32), xo_words[0].bitcast(I32))
        load_scales(xo_s, xo_scales, range(4))
        nc.sync.dma_start(ca_sb[3][:], ca_rows[:, 3, :])
        nc.sync.dma_start(lists["l5"][:], offs5)
        nc.sync.dma_start(w_w[:].bitcast(I32), w_words[0].bitcast(I32))
        load_scales(w_s, w_scales, range(4))
        nc.sync.dma_start(w0_w[:], w0_words[0].rearrange("p c r -> p (c r)").bitcast(I32))
        load_scales(w0_s, w0_scales, range(4))
        nc.sync.dma_start(wb_w[:], wb_words[0].rearrange("p c r -> p (c r)").bitcast(I32))
        load_scales(wb_s, wb_scales, range(4))

        codes = [tile([P, I], U8, "codes%d" % t) for t in range(PACK)]
        bars = [tile([P, I], F32, "bars%d" % t) for t in range(PACK)]
        picked = tile([P, PACK, J], F32, "picked")
        xt_wg = tile([P, J], U32, "xt_wg")
        xt_sg = tile([P, J], U8, "xt_sg")
        xo_wg = tile([P, J], U16, "xo_wg")
        xo_sg = tile([P, J], U8, "xo_sg")

        def look_up(t):
            nc.vector.tensor_copy(codes[t][:], ca_sb[t][:].indirect(lists["l3"][:]))

        def post_scalar(t):
            if t == 0:
                nc.scalar.activation(bars[t][:], codes[t][:].bitcast(FP8), COPY)
            else:
                nc.gpsimd.tensor_copy(bars[t][:], codes[t][:].bitcast(FP8))
            nc.scalar.activation(board[t][:].indirect(lists["l4"][:]), bars[t][:], COPY, scale=st_sb[:, t : t + 1])

        look_up(0)
        post_scalar(0)
        look_up(1)
        post_scalar(1)
        nc.vector.tensor_copy(xt_wg[:], xt_w[:].bitcast(U32).indirect(lists["l1"][:]))
        nc.vector.tensor_copy(xt_sg[:], xt_s[:].indirect(lists["l1"][:]))
        look_up(2)
        post_scalar(2)
        nc.vector.tensor_copy(xo_wg[:], xo_w[:].indirect(lists["l2"][:]))
        nc.vector.tensor_copy(xo_sg[:], xo_s[:].indirect(lists["l2"][:]))
        look_up(3)
        post_scalar(3)

        a_rows = [ps.tile([P, PACK, P], F32, name="a_rows%d" % h) for h in range(J // P)]
        halves = range(J // P)
        a_slots = [ps.tile([P, R], F32, name="a_slots%d" % h) for h in halves]
        for h in halves:
            cols = slice(h * P, (h + 1) * P)
            nc.tensor.matmul_mx(
                out=a_slots[h][:], lhsT=xt_wg[:, cols].bitcast(E4M3), lhsT_scale=xt_sg[:, cols],
                rhs=w_w[:].bitcast(E2M1), rhs_scale=w_s[:], start=True, stop=False,
            )
        for h in halves:
            cols = slice(h * P, (h + 1) * P)
            nc.tensor.matmul_mx(
                out=a_slots[h][:], lhsT=xo_wg[:, cols].bitcast(E2M1), lhsT_scale=xo_sg[:, cols],
                rhs=w0_w[:].bitcast(E5M2), rhs_scale=w0_s[:], start=False, stop=True,
            )
        dealt = [tile([P, PACK, P], F32, "dealt%d" % h) for h in halves]
        for h in halves:
            nc.vector.tensor_copy(dealt[h][:], a_slots[h][:].rearrange("j (p t) -> j t p", t=PACK))
            for t in range(PACK):
                nc.tensor.transpose(a_rows[h][:, t, :], dealt[h][:, t, :], ident[:])

        for t in range(PACK - 1):
            nc.vector.tensor_copy(picked[:, t, :], board[t][:].indirect(lists["l5"][:]))
        nc.scalar.activation(picked[:, PACK - 1, :], board[PACK - 1][:].indirect(lists["l5"][:]), COPY)
        diff = [tile([P, PACK, P], F32, "diff%d" % h) for h in halves]
        for h in halves:
            nc.vector.tensor_tensor(diff[h][:], a_rows[h][:], picked[:, :, h * P : (h + 1) * P], ALU.subtract)

        hid = [tile([P, P, PACK], BF16, "hid%d" % h) for h in halves]
        hid_w = [tile([P, P], U32, "hid_w%d" % h) for h in halves]
        hid_s = [tile([P, P], U8, "hid_s%d" % h) for h in halves]
        for h in halves:
            woven = hid[h][:].rearrange("p (c i) t -> p c t i", i=4)
            rows = diff[h][:].rearrange("p t (c i) -> p c t i", i=4)
            if h == 1:
                nc.vector.tensor_scalar(woven, rows, 0.0, None, ALU.max)
            else:
                nc.scalar.activation(woven, rows, RELU)
        for h in halves:
            nc.vector.quantize_mx(out=hid_w[h][:].bitcast(E4M3), scales=hid_s[h][:], in_=hid[h][:].rearrange("p j t -> p (j t)"))
        out_rows = out.rearrange("(g p) j -> p g j", p=P)
        for h in halves:
            acc = ps.tile([P, N // P, P], F32, name="acc%d" % h)
            for g in range(N // P):
                cols = slice(g * P, (g + 1) * P)
                nc.tensor.matmul_mx(
                    out=acc[:, g, :], lhsT=wb_w[:, cols].bitcast(E5M2), lhsT_scale=wb_s[:, cols],
                    rhs=hid_w[h][:].bitcast(E4M3), rhs_scale=hid_s[h][:], start=True, stop=True,
                )
            res = tile([P, N // P, P], F32, "res%d" % h)
            if h == 0:
                nc.scalar.copy(res[:], acc[:])
            else:
                nc.vector.tensor_copy(res[:], acc[:])
            nc.sync.dma_start(out_rows[:, :, h * P : (h + 1) * P], res[:])
